import numpy as np
import ml_dtypes


def mxq(x, axis, fmt="e4m3"):
    dtype, down = {"e4m3": (ml_dtypes.float8_e4m3fn, 7), "e5m2": (ml_dtypes.float8_e5m2, 14)}[fmt]
    v = np.moveaxis(np.asarray(x, np.float32).astype(ml_dtypes.bfloat16).astype(np.float64), axis, -1)
    blocks = v.reshape(v.shape[:-1] + (-1, 32))
    amax = np.abs(blocks).max(-1, keepdims=True)
    byte = np.maximum(np.where(amax > 0, np.frexp(amax)[1] - 1 + 127, 0) - down, 1)
    scale = np.exp2(byte - 127.0)
    codes = (blocks / scale).astype(np.float32).astype(dtype).astype(np.float64)
    return np.moveaxis((codes * scale).reshape(v.shape), -1, axis)


WIDE = False


def mx_kscale(k):
    if not WIDE:
        return np.ones(k)
    levels = np.array([10, -10, 5, -5, 0])
    if k % 512:
        return np.exp2(np.random.permutation(np.resize(levels, k // 32))).repeat(32)
    a = np.empty((k // 512, 16))
    for p in range(k // 512):
        a[p, :8] = np.random.permutation(np.resize(levels, 8))
        for g in range(8):
            far = levels[np.abs(levels - a[p, g]) >= 10]
            a[p, g + 8] = far[np.random.randint(len(far))]
    return np.exp2(a.ravel()).repeat(32)


def f64(x):
    return np.asarray(x).astype(np.float64)


def striped(idx):
    return np.tile(idx.reshape(-1, 16).T, (8, 1)).astype(np.uint16)


def unstriped(offs):
    return offs[:16].T.reshape(-1).astype(np.int64)


def striped8(idx):
    return np.concatenate([x.reshape(-1, 16).T for x in idx]).astype(np.uint16)


def runs(offs, k):
    lists = np.stack([offs[16 * r : 16 * r + 16].T.reshape(-1) for r in range(8)]).astype(np.int64)
    return lists[np.arange(k) % 512 // 64]


def pack_weight(w):
    k, n = w.shape
    w = f64(np.asarray(w, np.float32).astype(ml_dtypes.bfloat16)).reshape(k // 32, 32, n)
    amax = np.abs(w).max(1)
    byte = np.clip(np.where(amax > 0, np.frexp(amax)[1] - 1 + 127 - 7, 1), 1, 254)
    scaled = (w * np.exp2(127.0 - byte)[:, None, :]).reshape(k, n).astype(np.float32)
    words = np.ascontiguousarray(scaled.reshape(k // 512, 128, 4, n).transpose(0, 1, 3, 2)).astype(ml_dtypes.float8_e4m3fn).view(np.uint8)
    return words, np.ascontiguousarray(byte.astype(np.uint8).reshape(k // 512, 16, n))


def unpack_weight(words, scales):
    g, p, n, _ = words.shape
    vals = np.ascontiguousarray(words).view(ml_dtypes.float8_e4m3fn).astype(np.float64) * np.repeat(np.exp2(scales.astype(np.float64) - 127.0), 8, axis=1)[..., None]
    return vals.transpose(0, 1, 3, 2).reshape(g * 512, n)


E2M1 = np.array([0.0, 0.5, 1.0, 1.5, 2.0, 3.0, 4.0, 6.0, -0.0, -0.5, -1.0, -1.5, -2.0, -3.0, -4.0, -6.0])


def pack_fp4(w):
    k, n = w.shape
    w = f64(np.asarray(w, np.float32).astype(ml_dtypes.bfloat16)).reshape(k // 32, 32, n)
    amax = np.abs(w).max(1)
    mant, ex = np.frexp(amax / 6.0)
    byte = np.clip(np.where(amax > 0, np.where(mant > 0.5, ex, ex - 1) + 127, 1), 1, 254)
    scaled = (w * np.exp2(127.0 - byte)[:, None, :]).reshape(k, n).astype(np.float32)
    c = np.ascontiguousarray(scaled.reshape(k // 512, 128, 4, n).transpose(0, 1, 3, 2)).astype(ml_dtypes.float4_e2m1fn).view(np.uint8) & 0xF
    words = (c[..., 0::2] | (c[..., 1::2] << 4)).reshape(k // 512, 128, 2 * n)
    return np.ascontiguousarray(words), np.ascontiguousarray(byte.astype(np.uint8).reshape(k // 512, 16, n))


def unpack_fp4(words, scales):
    g, _, n = scales.shape
    words = np.ascontiguousarray(words).reshape(g, 128, n, 2)
    nib = np.empty((g, 128, n, 4), np.uint8)
    nib[..., 0::2] = words & 0xF
    nib[..., 1::2] = words >> 4
    vals = E2M1[nib] * np.repeat(np.exp2(scales.astype(np.float64) - 127.0), 8, axis=1)[..., None]
    return vals.transpose(0, 1, 3, 2).reshape(g * 512, n)


K, T, S, N, G, H, W, U = 512, 2048, 512, 512, 2048, 512, 256, 1024


def setup_inputs():
    n = np.random.standard_normal
    s = mx_kscale(K)[:, None]
    u = mx_kscale(S)
    packed_xT = pack_weight(n((K, T)) * s)
    packed_dT = pack_weight(n((K, G)) / s)
    packed_w1 = pack_fp4(n((H, N)) / np.sqrt(H) / u[:, None])
    perm = np.stack([np.random.permutation(S) for _ in range(8)])
    perm2 = np.stack([np.random.permutation(U) for _ in range(8)])
    return {
        "x_words": packed_xT[0],
        "x_scales": packed_xT[1],
        "d_words": packed_dT[0],
        "d_scales": packed_dT[1],
        "gn": (np.random.uniform(0.5, 1.5, (H, 1)) * u[:, None]).astype(np.float32),
        "w1_words": packed_w1[0],
        "w1_scales": packed_w1[1],
        "offs": striped(np.random.permutation(T)[:S]),
        "kidx": striped8(np.random.randint(0, G, (8, H))),
        "n1": striped8(perm[:, :W]),
        "n2": striped8(perm[:, W:]),
        "n3": striped8(perm2[:, :S]),
        "n4": striped8(perm2[:, S:]),
        "n5": striped8(np.stack([np.random.permutation(S) for _ in range(8)])),
    }


def reference(x_words, x_scales, d_words, d_scales, gn, w1_words, w1_scales, offs, kidx, n1, n2, n3, n4, n5):
    d_kidx = unpack_weight(d_words, d_scales)[np.arange(K)[:, None], runs(kidx, K)]
    xq = unpack_weight(x_words, x_scales)[:, unstriped(offs)]
    s = 0.0625 * (d_kidx.T @ xq)
    pa = s[np.arange(H)[:, None], runs(n1, H)]
    pb = s[np.arange(H)[:, None], runs(n2, H)]
    ra = np.maximum(pa, pb)
    ds = s.copy()
    ds[np.arange(H)[:, None], runs(n1, H)] = ra
    z = f64(gn) * ds
    h = unpack_fp4(w1_words, w1_scales).T @ mxq(z, 0, "e4m3")
    nw = h - (h[np.arange(N)[:, None], runs(n5, N)])
    ph = np.zeros((N, U))
    ph[np.arange(N)[:, None], runs(n3, N)] = h
    out = ph.copy()
    out[np.arange(N)[:, None], runs(n4, N)] = nw
    return out

@@ -1,0 +1,204 @@
+from contextlib import ExitStack
+
+import concourse.mybir as mybir
+
+FLOPS = 536870912
+
+F32 = mybir.dt.float32
+BF16 = mybir.dt.bfloat16
+I32 = mybir.dt.int32
+U32 = mybir.dt.uint32
+U16 = mybir.dt.uint16
+U8 = mybir.dt.uint8
+FP8X4 = mybir.dt.float8_e4m3fn_x4
+FP4X4 = mybir.dt.float4_e2m1fn_x4
+COPY = mybir.ActivationFunctionType.Copy
+ALU = mybir.AluOpType
+
+P = 128
+PACK = 4
+TABLE = 2048
+S = 512
+W = 256
+U = 1024
+CH = 128
+
+
+def tile_picked_keyfillpagq_none_p_kernel(
+    tc, x_words, x_scales, d_words, d_scales, gn, w1_words, w1_scales, offs, kidx, n1, n2, n3, n4, n5, out
+):
+    nc = tc.nc
+    with ExitStack() as ctx:
+        lists = ctx.enter_context(tc.tile_pool(name="lists", bufs=1))
+        keep = ctx.enter_context(tc.tile_pool(name="keep", bufs=1))
+        psum = ctx.enter_context(tc.psum_pool(name="psum", bufs=1))
+
+        def sb(name, shape, dtype, tag=""):
+            return keep.tile(shape, dtype, name=name, tag=tag or name, align_bytes=64)
+
+        def load_list(name, src):
+            t = lists.tile([P, src.shape[1]], U16, name=name)
+            nc.sync.dma_start(t[:], src)
+            return t
+
+        banks = [psum.tile([P, S], F32, name="bank%d" % b) for b in range(8)]
+
+        d_win = sb("d_win", [P, TABLE], U32)
+        x_win = sb("x_win", [P, TABLE], U32)
+        ds_win = sb("ds_win", [P, TABLE], U8)
+        xs_win = sb("xs_win", [P, TABLE], U8)
+        d_plane = sb("d_plane", [P, S], U8)
+        gn_raw = sb("gn_raw", [P, PACK], F32)
+
+        nc.gpsimd.memset(ds_win[:].bitcast(I32), 0)
+        nc.vector.memset(xs_win[:].bitcast(I32), 0)
+        nc.vector.memset(d_plane[:].bitcast(I32), 0)
+
+        nc.gpsimd.dma_start(ds_win[0:P:8, :].bitcast(I32), d_scales[0].bitcast(I32))
+        xs_rows = x_scales[0].rearrange("(q a) c -> a q c", a=4)
+        for a in range(4):
+            nc.gpsimd.dma_start(xs_win[a:P:32, :].bitcast(I32), xs_rows[a].bitcast(I32))
+        nc.scalar.dma_start(gn_raw[:], gn.rearrange("(p t) o -> p (t o)", t=PACK))
+        kidx_t = load_list("kidx_t", kidx)
+        nc.sync.dma_start(d_win[:].bitcast(I32), d_words[0].rearrange("p n t -> p (n t)").bitcast(I32))
+        offs_t = load_list("offs_t", offs)
+        n1_t = load_list("n1_t", n1)
+        n2_t = load_list("n2_t", n2)
+        nc.sync.dma_start(x_win[:].bitcast(I32), x_words[0].rearrange("p n t -> p (n t)").bitcast(I32))
+        n3_t = load_list("n3_t", n3)
+        n5_t = load_list("n5_t", n5)
+        n4_t = load_list("n4_t", n4)
+
+        ds_got = sb("ds_got", [P, S], U8)
+        ds_dealt = sb("ds_dealt", [P, S], U8)
+        nc.vector.tensor_copy(ds_got[:], ds_win[:].indirect(kidx_t[:]))
+        nc.vector.tensor_copy(
+            ds_dealt[:].rearrange("p (t q) -> p t q", t=PACK), ds_got[:].rearrange("p (q t) -> p t q", t=PACK)
+        )
+        for a in range(4):
+            nc.scalar.dma_start(d_plane[a:P:32, :].bitcast(I32), ds_dealt[8 * a : P : 32, :].bitcast(I32))
+
+        d_got = sb("d_got", [P, S], U32)
+        d_codes = sb("d_codes", [P, S], U32)
+        nc.vector.tensor_copy(d_got[:], d_win[:].indirect(kidx_t[:]))
+        nc.vector.tensor_copy(
+            d_codes[:].rearrange("p (t q) -> p t q", t=PACK), d_got[:].rearrange("p (q t) -> p t q", t=PACK)
+        )
+
+        x_plane = sb("x_plane", [P, S], U8)
+        nc.vector.tensor_copy(x_plane[:], xs_win[:].indirect(offs_t[:]))
+
+        ws_raw = sb("ws_raw", [P, S], U8, tag="d_win")
+        w_raw = sb("w_raw", [P, 2 * S], U8, tag="d_got")
+        nc.gpsimd.memset(ws_raw[:].bitcast(I32), 0)
+        ws_rows = w1_scales[0].rearrange("(q a) c -> a q c", a=4)
+        for a in range(4):
+            nc.sync.dma_start(ws_raw[a:P:32, :].bitcast(I32), ws_rows[a].bitcast(I32))
+        nc.sync.dma_start(w_raw[:].bitcast(I32), w1_words[0].bitcast(I32))
+
+        gain = sb("gain", [P, PACK], F32)
+        nc.scalar.activation(gain[:], gn_raw[:], COPY, scale=0.0625)
+
+        x_codes = sb("x_codes", [P, S], U32)
+        scores = [sb("score%d" % t, [P, S], F32) for t in range(PACK)]
+
+        def score_matmul(bank, t, cols):
+            keys = slice(t * P, (t + 1) * P)
+            nc.tensor.matmul_mx(
+                out=bank, lhsT=d_codes[:, keys].bitcast(FP8X4), lhsT_scale=d_plane[:, keys],
+                rhs=x_codes[:, cols].bitcast(FP8X4), rhs_scale=x_plane[:, cols], start=True, stop=True,
+            )
+
+        for half in range(2):
+            cols = slice(half * W, (half + 1) * W)
+            nc.vector.tensor_copy(x_codes[:, cols], x_win[:].indirect(offs_t[:, half * 16 : (half + 1) * 16]))
+            score_matmul(banks[half][:, 0:W], 0, cols)
+            nc.scalar.copy(scores[0][:, cols], banks[half][:, 0:W])
+        for t in range(1, PACK):
+            score_matmul(banks[1 + t][:], t, slice(0, S))
+
+        for t in range(PACK):
+            if t > 0:
+                nc.scalar.copy(scores[t][:], banks[1 + t][:])
+            pa = sb("pa%d" % t, [P, W], F32)
+            pb = sb("pb%d" % t, [P, W], F32)
+            ra = sb("ra%d" % t, [P, W], F32)
+            nc.scalar.activation(pa[:], scores[t][:].indirect(n1_t[:]), COPY)
+            if t == 0:
+                nc.vector.tensor_copy(pb[:], scores[t][:].indirect(n2_t[:]))
+            else:
+                nc.scalar.activation(pb[:], scores[t][:].indirect(n2_t[:]), COPY)
+            nc.vector.tensor_tensor(ra[:], pa[:], pb[:], ALU.max)
+            nc.vector.tensor_copy(scores[t][:].indirect(n1_t[:]), ra[:])
+
+        pages = []
+        for t, tag in enumerate(("x_win", "pb0", "pa1", "pa2")):
+            pages.append(sb("page%d" % t, [P, U], F32, tag=tag))
+            nc.gpsimd.memset(pages[t][:], 0.0)
+
+        w_codes = sb("w_codes", [P, 2 * S], U8)
+        w_plane = sb("w_plane", [P, S], U8)
+        nc.vector.tensor_copy(
+            w_plane[:].rearrange("p (t q) -> p t q", t=PACK), ws_raw[:].rearrange("p (q t) -> p t q", t=PACK)
+        )
+        nc.scalar.copy(
+            w_codes[:].bitcast(U16).rearrange("p (t q) -> p t q", t=PACK),
+            w_raw[:].bitcast(U16).rearrange("p (q t) -> p t q", t=PACK),
+        )
+
+        z_woven = [sb("z_woven%d" % c, [P, CH, PACK], BF16) for c in range(S // CH)]
+        z_rest = sb("z_rest", [P, PACK, S - CH], BF16)
+        for t in range(PACK):
+            g = gain[:, t : t + 1]
+            if t < 2:
+                nc.scalar.activation(z_woven[0][:, :, t], scores[t][:, 0:CH], COPY, scale=g)
+            else:
+                nc.vector.tensor_scalar(z_woven[0][:, :, t], scores[t][:, 0:CH], g, None, ALU.mult)
+            nc.scalar.activation(z_rest[:, t, :], scores[t][:, CH:S], COPY, scale=g)
+
+        z_codes = sb("z_codes", [P, S], U32)
+        z_plane = sb("z_plane", [P, S], U8)
+        sums = [sb("sum%d" % t, [P, S], F32) for t in range(PACK)]
+
+        def value_matmul(bank, t, cols):
+            nc.tensor.matmul_mx(
+                out=bank, lhsT=w_codes[:, 2 * t * P : 2 * (t + 1) * P].bitcast(FP4X4),
+                lhsT_scale=w_plane[:, t * P : (t + 1) * P],
+                rhs=z_codes[:, cols].bitcast(FP8X4), rhs_scale=z_plane[:, cols], start=True, stop=True,
+            )
+
+        for c in range(S // CH):
+            cols = slice(c * CH, (c + 1) * CH)
+            if c > 0:
+                nc.scalar.copy(
+                    z_woven[c][:].rearrange("p (j i) t -> p j t i", i=4),
+                    z_rest[:, :, (c - 1) * CH : c * CH].rearrange("p t (j i) -> p j t i", i=4),
+                )
+            nc.vector.quantize_mx(
+                out=z_codes[:, cols].bitcast(FP8X4), scales=z_plane[:, cols],
+                in_=z_woven[c][:].rearrange("p j t -> p (j t)"),
+            )
+            bank = banks[(5 + c) % 8][:, 0:CH]
+            value_matmul(bank, 0, cols)
+            nc.scalar.copy(sums[0][:, cols], bank)
+            nc.vector.tensor_copy(pages[0][:].indirect(n3_t[:, c * 8 : (c + 1) * 8]), sums[0][:, cols])
+        for t in range(1, PACK):
+            value_matmul(banks[t][:], t, slice(0, S))
+
+        out_rows = out.rearrange("(p t) w -> t p w", t=PACK)
+
+        def second_fill(t):
+            minus = sb("minus%d" % t, [P, S], F32)
+            for half in range(2):
+                nc.scalar.activation(
+                    minus[:, half * W : (half + 1) * W],
+                    sums[t][:].indirect(n5_t[:, half * 16 : (half + 1) * 16]), COPY, scale=-1.0,
+                )
+            nc.vector.tensor_tensor(pages[t][:].indirect(n4_t[:]), sums[t][:], minus[:], ALU.add)
+            nc.sync.dma_start(out_rows[t], pages[t][:])
+
+        for t in range(1, PACK):
+            nc.scalar.copy(sums[t][:], banks[t][:])
+            nc.vector.tensor_copy(pages[t][:].indirect(n3_t[:]), sums[t][:])
+            second_fill(t - 1)
+        second_fill(PACK - 1)

@@ -47,54 +47,52 @@ def tile_picked_keyfillpagq_none_p_kernel(
         x_win = sb("x_win", [P, TABLE], U32)
         ds_win = sb("ds_win", [P, TABLE], U8)
         xs_win = sb("xs_win", [P, TABLE], U8)
-        d_plane = sb("d_plane", [P, S], U8)
         gn_raw = sb("gn_raw", [P, PACK], F32)
+        ws_raw = sb("ws_raw", [P, S], U8)
+        w_raw = sb("w_raw", [P, 2 * S], U8)
 
         nc.gpsimd.memset(ds_win[:].bitcast(I32), 0)
         nc.vector.memset(xs_win[:].bitcast(I32), 0)
-        nc.vector.memset(d_plane[:].bitcast(I32), 0)
+        nc.gpsimd.memset(ws_raw[:].bitcast(I32), 0)
 
-        nc.gpsimd.dma_start(ds_win[0:P:8, :].bitcast(I32), d_scales[0].bitcast(I32))
-        xs_rows = x_scales[0].rearrange("(q a) c -> a q c", a=4)
-        for a in range(4):
-            nc.gpsimd.dma_start(xs_win[a:P:32, :].bitcast(I32), xs_rows[a].bitcast(I32))
-        nc.scalar.dma_start(gn_raw[:], gn.rearrange("(p t) o -> p (t o)", t=PACK))
+        nc.scalar.dma_start(ds_win[0:P:8, :].bitcast(I32), d_scales[0].bitcast(I32))
+        nc.scalar.dma_start(xs_win[0:P:8, :].bitcast(I32), x_scales[0].bitcast(I32))
         kidx_t = load_list("kidx_t", kidx)
-        nc.sync.dma_start(d_win[:].bitcast(I32), d_words[0].rearrange("p n t -> p (n t)").bitcast(I32))
         offs_t = load_list("offs_t", offs)
+        nc.sync.dma_start(d_win[:].bitcast(I32), d_words[0].rearrange("p n t -> p (n t)").bitcast(I32))
         n1_t = load_list("n1_t", n1)
         n2_t = load_list("n2_t", n2)
-        nc.sync.dma_start(x_win[:].bitcast(I32), x_words[0].rearrange("p n t -> p (n t)").bitcast(I32))
         n3_t = load_list("n3_t", n3)
         n5_t = load_list("n5_t", n5)
+        nc.sync.dma_start(x_win[:].bitcast(I32), x_words[0].rearrange("p n t -> p (n t)").bitcast(I32))
         n4_t = load_list("n4_t", n4)
+        nc.gpsimd.dma_start(w_raw[:].bitcast(I32), w1_words[0].bitcast(I32))
+        nc.gpsimd.dma_start(gn_raw[:], gn.rearrange("(p t) o -> p (t o)", t=PACK))
+        for q in range(4):
+            nc.gpsimd.dma_start(ws_raw[32 * q : 32 * q + 4, :].bitcast(I32), w1_scales[0, 4 * q : 4 * q + 4, :].bitcast(I32))
 
+        staged = sb("staged", [P, 2 * S], U8)
+        planes = sb("planes", [P, 2 * S], U8)
+        nc.vector.memset(planes[:].bitcast(I32), 0)
+        d_plane = planes[:, 0:S]
+        x_plane = planes[:, S : 2 * S]
         ds_got = sb("ds_got", [P, S], U8)
-        ds_dealt = sb("ds_dealt", [P, S], U8)
         nc.vector.tensor_copy(ds_got[:], ds_win[:].indirect(kidx_t[:]))
+        xs_got = sb("xs_got", [P, S], U8)
+        nc.vector.tensor_copy(xs_got[:], xs_win[:].indirect(offs_t[:]))
         nc.vector.tensor_copy(
-            ds_dealt[:].rearrange("p (t q) -> p t q", t=PACK), ds_got[:].rearrange("p (q t) -> p t q", t=PACK)
+            staged[:, 0:S].rearrange("p (t q) -> p t q", t=PACK), ds_got[:].rearrange("p (q t) -> p t q", t=PACK)
         )
-        for a in range(4):
-            nc.scalar.dma_start(d_plane[a:P:32, :].bitcast(I32), ds_dealt[8 * a : P : 32, :].bitcast(I32))
+        nc.vector.tensor_copy(staged[:, S : 2 * S].bitcast(I32), xs_got[:].bitcast(I32))
+        for q in range(4):
+            queue = nc.sync if q % 2 == 0 else nc.scalar
+            queue.dma_start(planes[32 * q : 32 * q + 4, :].bitcast(I32), staged[32 * q : 32 * (q + 1) : 8, :].bitcast(I32))
 
         d_got = sb("d_got", [P, S], U32)
         d_codes = sb("d_codes", [P, S], U32)
         nc.vector.tensor_copy(d_got[:], d_win[:].indirect(kidx_t[:]))
-        nc.vector.tensor_copy(
-            d_codes[:].rearrange("p (t q) -> p t q", t=PACK), d_got[:].rearrange("p (q t) -> p t q", t=PACK)
-        )
-
-        x_plane = sb("x_plane", [P, S], U8)
-        nc.vector.tensor_copy(x_plane[:], xs_win[:].indirect(offs_t[:]))
-
-        ws_raw = sb("ws_raw", [P, S], U8, tag="d_win")
-        w_raw = sb("w_raw", [P, 2 * S], U8, tag="d_got")
-        nc.gpsimd.memset(ws_raw[:].bitcast(I32), 0)
-        ws_rows = w1_scales[0].rearrange("(q a) c -> a q c", a=4)
-        for a in range(4):
-            nc.sync.dma_start(ws_raw[a:P:32, :].bitcast(I32), ws_rows[a].bitcast(I32))
-        nc.sync.dma_start(w_raw[:].bitcast(I32), w1_words[0].bitcast(I32))
+        dealt = d_codes[:].rearrange("p (t q) -> p t q", t=PACK)
+        picked = d_got[:].rearrange("p (q t) -> p t q", t=PACK)
 
         gain = sb("gain", [P, PACK], F32)
         nc.scalar.activation(gain[:], gn_raw[:], COPY, scale=0.0625)
@@ -109,17 +107,20 @@ def tile_picked_keyfillpagq_none_p_kernel(
                 rhs=x_codes[:, cols].bitcast(FP8X4), rhs_scale=x_plane[:, cols], start=True, stop=True,
             )
 
-        for half in range(2):
-            cols = slice(half * W, (half + 1) * W)
-            nc.vector.tensor_copy(x_codes[:, cols], x_win[:].indirect(offs_t[:, half * 16 : (half + 1) * 16]))
-            score_matmul(banks[half][:, 0:W], 0, cols)
-            nc.scalar.copy(scores[0][:, cols], banks[half][:, 0:W])
-        for t in range(1, PACK):
-            score_matmul(banks[1 + t][:], t, slice(0, S))
+        chunks = (slice(0, 2 * CH), slice(2 * CH, 3 * CH), slice(3 * CH, S))
+        for c, cols in enumerate(chunks):
+            nc.vector.tensor_copy(x_codes[:, cols], x_win[:].indirect(offs_t[:, cols.start // 16 : cols.stop // 16]))
+            if c == 0:
+                nc.vector.tensor_copy(dealt[:, 0, :], picked[:, 0, :])
+            bank = banks[c][:, 0 : cols.stop - cols.start]
+            score_matmul(bank, 0, cols)
+            nc.scalar.copy(scores[0][:, cols], bank)
+        nc.vector.tensor_copy(dealt[:, 1:PACK, :], picked[:, 1:PACK, :])
 
         for t in range(PACK):
             if t > 0:
-                nc.scalar.copy(scores[t][:], banks[1 + t][:])
+                score_matmul(banks[2][:], t, slice(0, S))
+                nc.scalar.copy(scores[t][:], banks[2][:])
             pa = sb("pa%d" % t, [P, W], F32)
             pb = sb("pb%d" % t, [P, W], F32)
             ra = sb("ra%d" % t, [P, W], F32)
@@ -132,13 +133,12 @@ def tile_picked_keyfillpagq_none_p_kernel(
             nc.vector.tensor_copy(scores[t][:].indirect(n1_t[:]), ra[:])
 
         pages = []
-        for t, tag in enumerate(("x_win", "pb0", "pa1", "pa2")):
-            pages.append(sb("page%d" % t, [P, U], F32, tag=tag))
-            nc.gpsimd.memset(pages[t][:], 0.0)
+        for t in range(PACK):
+            pages.append(sb("page%d" % t, [P, U], F32))
 
         w_codes = sb("w_codes", [P, 2 * S], U8)
         w_plane = sb("w_plane", [P, S], U8)
-        nc.vector.tensor_copy(
+        nc.gpsimd.tensor_copy(
             w_plane[:].rearrange("p (t q) -> p t q", t=PACK), ws_raw[:].rearrange("p (q t) -> p t q", t=PACK)
         )
         nc.scalar.copy(
@@ -146,8 +146,12 @@ def tile_picked_keyfillpagq_none_p_kernel(
             w_raw[:].bitcast(U16).rearrange("p (q t) -> p t q", t=PACK),
         )
 
-        z_woven = [sb("z_woven%d" % c, [P, CH, PACK], BF16) for c in range(S // CH)]
-        z_rest = sb("z_rest", [P, PACK, S - CH], BF16)
+        chunks = (slice(0, CH), slice(CH, 2 * CH), slice(2 * CH, S))
+        z_woven = [
+            sb("z_woven%d" % c, [P, cols.stop - cols.start, PACK], BF16, tag="pb2" if c == 0 else "")
+            for c, cols in enumerate(chunks)
+        ]
+        z_rest = sb("z_rest", [P, PACK, S - CH], BF16, tag="pa2")
         for t in range(PACK):
             g = gain[:, t : t + 1]
             if t < 2:
@@ -167,23 +171,24 @@ def tile_picked_keyfillpagq_none_p_kernel(
                 rhs=z_codes[:, cols].bitcast(FP8X4), rhs_scale=z_plane[:, cols], start=True, stop=True,
             )
 
-        for c in range(S // CH):
-            cols = slice(c * CH, (c + 1) * CH)
+        for c, cols in enumerate(chunks):
             if c > 0:
                 nc.scalar.copy(
                     z_woven[c][:].rearrange("p (j i) t -> p j t i", i=4),
-                    z_rest[:, :, (c - 1) * CH : c * CH].rearrange("p t (j i) -> p j t i", i=4),
+                    z_rest[:, :, cols.start - CH : cols.stop - CH].rearrange("p t (j i) -> p j t i", i=4),
                 )
             nc.vector.quantize_mx(
                 out=z_codes[:, cols].bitcast(FP8X4), scales=z_plane[:, cols],
                 in_=z_woven[c][:].rearrange("p j t -> p (j t)"),
             )
-            bank = banks[(5 + c) % 8][:, 0:CH]
-            value_matmul(bank, 0, cols)
-            nc.scalar.copy(sums[0][:, cols], bank)
-            nc.vector.tensor_copy(pages[0][:].indirect(n3_t[:, c * 8 : (c + 1) * 8]), sums[0][:, cols])
-        for t in range(1, PACK):
-            value_matmul(banks[t][:], t, slice(0, S))
+            for t in range(2):
+                bank = banks[2 + 2 * c + t][:, 0 : cols.stop - cols.start]
+                value_matmul(bank, t, cols)
+                if c == 0 and t == 0:
+                    nc.vector.tensor_copy(sums[t][:, cols], bank)
+                else:
+                    nc.scalar.copy(sums[t][:, cols], bank)
+                nc.vector.tensor_copy(pages[t][:].indirect(n3_t[:, cols.start // 16 : cols.stop // 16]), sums[t][:, cols])
 
         out_rows = out.rearrange("(p t) w -> t p w", t=PACK)
 
@@ -197,8 +202,10 @@ def tile_picked_keyfillpagq_none_p_kernel(
             nc.vector.tensor_tensor(pages[t][:].indirect(n4_t[:]), sums[t][:], minus[:], ALU.add)
             nc.sync.dma_start(out_rows[t], pages[t][:])
 
-        for t in range(1, PACK):
-            nc.scalar.copy(sums[t][:], banks[t][:])
+        for t in range(2, PACK):
+            second_fill(t - 2)
+            value_matmul(banks[t - 2][:], t, slice(0, S))
+            nc.scalar.copy(sums[t][:], banks[t - 2][:])
             nc.vector.tensor_copy(pages[t][:].indirect(n3_t[:]), sums[t][:])
-            second_fill(t - 1)
-        second_fill(PACK - 1)
+        second_fill(2)
+        second_fill(3)

@@ -55,16 +55,16 @@ def tile_picked_keyfillpagq_none_p_kernel(
         nc.vector.memset(xs_win[:].bitcast(I32), 0)
         nc.gpsimd.memset(ws_raw[:].bitcast(I32), 0)
 
-        nc.scalar.dma_start(ds_win[0:P:8, :].bitcast(I32), d_scales[0].bitcast(I32))
-        nc.scalar.dma_start(xs_win[0:P:8, :].bitcast(I32), x_scales[0].bitcast(I32))
         kidx_t = load_list("kidx_t", kidx)
+        nc.sync.dma_start(ds_win[0:P:8, :].bitcast(I32), d_scales[0].bitcast(I32))
+        nc.sync.dma_start(xs_win[0:P:8, :].bitcast(I32), x_scales[0].bitcast(I32))
         offs_t = load_list("offs_t", offs)
-        nc.sync.dma_start(d_win[:].bitcast(I32), d_words[0].rearrange("p n t -> p (n t)").bitcast(I32))
         n1_t = load_list("n1_t", n1)
         n2_t = load_list("n2_t", n2)
         n3_t = load_list("n3_t", n3)
-        n5_t = load_list("n5_t", n5)
+        nc.sync.dma_start(d_win[:].bitcast(I32), d_words[0].rearrange("p n t -> p (n t)").bitcast(I32))
         nc.sync.dma_start(x_win[:].bitcast(I32), x_words[0].rearrange("p n t -> p (n t)").bitcast(I32))
+        n5_t = load_list("n5_t", n5)
         n4_t = load_list("n4_t", n4)
         nc.gpsimd.dma_start(w_raw[:].bitcast(I32), w1_words[0].bitcast(I32))
         nc.gpsimd.dma_start(gn_raw[:], gn.rearrange("(p t) o -> p (t o)", t=PACK))
@@ -81,7 +81,7 @@ def tile_picked_keyfillpagq_none_p_kernel(
         xs_got = sb("xs_got", [P, S], U8)
         nc.vector.tensor_copy(xs_got[:], xs_win[:].indirect(offs_t[:]))
         nc.vector.tensor_copy(
-            staged[:, 0:S].rearrange("p (t q) -> p t q", t=PACK), ds_got[:].rearrange("p (q t) -> p t q", t=PACK)
+            staged[:, 0:S].rearrange("p (t q) -> p q t", t=PACK), ds_got[:].rearrange("p (q t) -> p q t", t=PACK)
         )
         nc.vector.tensor_copy(staged[:, S : 2 * S].bitcast(I32), xs_got[:].bitcast(I32))
         for q in range(4):
@@ -91,8 +91,8 @@ def tile_picked_keyfillpagq_none_p_kernel(
         d_got = sb("d_got", [P, S], U32)
         d_codes = sb("d_codes", [P, S], U32)
         nc.vector.tensor_copy(d_got[:], d_win[:].indirect(kidx_t[:]))
-        dealt = d_codes[:].rearrange("p (t q) -> p t q", t=PACK)
-        picked = d_got[:].rearrange("p (q t) -> p t q", t=PACK)
+        dealt = d_codes[:].rearrange("p (t q) -> p q t", t=PACK)
+        picked = d_got[:].rearrange("p (q t) -> p q t", t=PACK)
 
         gain = sb("gain", [P, PACK], F32)
         nc.scalar.activation(gain[:], gn_raw[:], COPY, scale=0.0625)
@@ -111,11 +111,11 @@ def tile_picked_keyfillpagq_none_p_kernel(
         for c, cols in enumerate(chunks):
             nc.vector.tensor_copy(x_codes[:, cols], x_win[:].indirect(offs_t[:, cols.start // 16 : cols.stop // 16]))
             if c == 0:
-                nc.vector.tensor_copy(dealt[:, 0, :], picked[:, 0, :])
+                nc.vector.tensor_copy(dealt[:, :, 0], picked[:, :, 0])
             bank = banks[c][:, 0 : cols.stop - cols.start]
             score_matmul(bank, 0, cols)
             nc.scalar.copy(scores[0][:, cols], bank)
-        nc.vector.tensor_copy(dealt[:, 1:PACK, :], picked[:, 1:PACK, :])
+        nc.vector.tensor_copy(dealt[:, :, 1:PACK], picked[:, :, 1:PACK])
 
         for t in range(PACK):
             if t > 0:
@@ -148,16 +148,13 @@ def tile_picked_keyfillpagq_none_p_kernel(
 
         chunks = (slice(0, CH), slice(CH, 2 * CH), slice(2 * CH, S))
         z_woven = [
-            sb("z_woven%d" % c, [P, cols.stop - cols.start, PACK], BF16, tag="pb2" if c == 0 else "")
+            sb("z_woven%d" % c, [P, cols.stop - cols.start, PACK], BF16, tag="pb1" if c == 0 else "")
             for c, cols in enumerate(chunks)
         ]
         z_rest = sb("z_rest", [P, PACK, S - CH], BF16, tag="pa2")
         for t in range(PACK):
             g = gain[:, t : t + 1]
-            if t < 2:
-                nc.scalar.activation(z_woven[0][:, :, t], scores[t][:, 0:CH], COPY, scale=g)
-            else:
-                nc.vector.tensor_scalar(z_woven[0][:, :, t], scores[t][:, 0:CH], g, None, ALU.mult)
+            nc.scalar.activation(z_woven[0][:, :, t], scores[t][:, 0:CH], COPY, scale=g)
             nc.scalar.activation(z_rest[:, t, :], scores[t][:, CH:S], COPY, scale=g)
 
         z_codes = sb("z_codes", [P, S], U32)

@@ -61,15 +61,15 @@ def tile_picked_keyfillpagq_none_p_kernel(
         offs_t = load_list("offs_t", offs)
         n1_t = load_list("n1_t", n1)
         n2_t = load_list("n2_t", n2)
-        n3_t = load_list("n3_t", n3)
+        nc.sync.dma_start(gn_raw[:], gn.rearrange("(p t) o -> p (t o)", t=PACK))
         nc.sync.dma_start(d_win[:].bitcast(I32), d_words[0].rearrange("p n t -> p (n t)").bitcast(I32))
         nc.sync.dma_start(x_win[:].bitcast(I32), x_words[0].rearrange("p n t -> p (n t)").bitcast(I32))
+        nc.sync.dma_start(w_raw[:].bitcast(I32), w1_words[0].bitcast(I32))
+        for q in range(4):
+            nc.sync.dma_start(ws_raw[32 * q : 32 * q + 4, :].bitcast(I32), w1_scales[0, 4 * q : 4 * q + 4, :].bitcast(I32))
+        n3_t = load_list("n3_t", n3)
         n5_t = load_list("n5_t", n5)
         n4_t = load_list("n4_t", n4)
-        nc.gpsimd.dma_start(w_raw[:].bitcast(I32), w1_words[0].bitcast(I32))
-        nc.gpsimd.dma_start(gn_raw[:], gn.rearrange("(p t) o -> p (t o)", t=PACK))
-        for q in range(4):
-            nc.gpsimd.dma_start(ws_raw[32 * q : 32 * q + 4, :].bitcast(I32), w1_scales[0, 4 * q : 4 * q + 4, :].bitcast(I32))
 
         staged = sb("staged", [P, 2 * S], U8)
         planes = sb("planes", [P, 2 * S], U8)
@@ -85,8 +85,7 @@ def tile_picked_keyfillpagq_none_p_kernel(
         )
         nc.vector.tensor_copy(staged[:, S : 2 * S].bitcast(I32), xs_got[:].bitcast(I32))
         for q in range(4):
-            queue = nc.sync if q % 2 == 0 else nc.scalar
-            queue.dma_start(planes[32 * q : 32 * q + 4, :].bitcast(I32), staged[32 * q : 32 * (q + 1) : 8, :].bitcast(I32))
+            nc.scalar.dma_start(planes[32 * q : 32 * q + 4, :].bitcast(I32), staged[32 * q : 32 * (q + 1) : 8, :].bitcast(I32))
 
         d_got = sb("d_got", [P, S], U32)
         d_codes = sb("d_codes", [P, S], U32)
@@ -116,6 +115,10 @@ def tile_picked_keyfillpagq_none_p_kernel(
             score_matmul(bank, 0, cols)
             nc.scalar.copy(scores[0][:, cols], bank)
         nc.vector.tensor_copy(dealt[:, :, 1:PACK], picked[:, :, 1:PACK])
+        w_plane = sb("w_plane", [P, S], U8, tag="x_win")
+        nc.vector.tensor_copy(
+            w_plane[:].rearrange("p (t q) -> p q t", t=PACK), ws_raw[:].rearrange("p (q t) -> p q t", t=PACK)
+        )
 
         for t in range(PACK):
             if t > 0:
@@ -137,10 +140,6 @@ def tile_picked_keyfillpagq_none_p_kernel(
             pages.append(sb("page%d" % t, [P, U], F32))
 
         w_codes = sb("w_codes", [P, 2 * S], U8)
-        w_plane = sb("w_plane", [P, S], U8)
-        nc.gpsimd.tensor_copy(
-            w_plane[:].rearrange("p (t q) -> p t q", t=PACK), ws_raw[:].rearrange("p (q t) -> p t q", t=PACK)
-        )
         nc.scalar.copy(
             w_codes[:].bitcast(U16).rearrange("p (t q) -> p t q", t=PACK),
             w_raw[:].bitcast(U16).rearrange("p (q t) -> p t q", t=PACK),

from contextlib import ExitStack

import concourse.mybir as mybir

FLOPS = 536870912

F32 = mybir.dt.float32
BF16 = mybir.dt.bfloat16
I32 = mybir.dt.int32
U32 = mybir.dt.uint32
U16 = mybir.dt.uint16
U8 = mybir.dt.uint8
FP8X4 = mybir.dt.float8_e4m3fn_x4
FP4X4 = mybir.dt.float4_e2m1fn_x4
COPY = mybir.ActivationFunctionType.Copy
ALU = mybir.AluOpType

P = 128
PACK = 4
TABLE = 2048
S = 512
W = 256
U = 1024
CH = 128


def tile_picked_keyfillpagq_none_p_kernel(
    tc, x_words, x_scales, d_words, d_scales, gn, w1_words, w1_scales, offs, kidx, n1, n2, n3, n4, n5, out
):
    nc = tc.nc
    with ExitStack() as ctx:
        lists = ctx.enter_context(tc.tile_pool(name="lists", bufs=1))
        keep = ctx.enter_context(tc.tile_pool(name="keep", bufs=1))
        psum = ctx.enter_context(tc.psum_pool(name="psum", bufs=1))

        def sb(name, shape, dtype, tag=""):
            return keep.tile(shape, dtype, name=name, tag=tag or name, align_bytes=64)

        def load_list(name, src):
            t = lists.tile([P, src.shape[1]], U16, name=name)
            nc.sync.dma_start(t[:], src)
            return t

        banks = [psum.tile([P, S], F32, name="bank%d" % b) for b in range(8)]

        d_win = sb("d_win", [P, TABLE], U32)
        x_win = sb("x_win", [P, TABLE], U32)
        ds_win = sb("ds_win", [P, TABLE], U8)
        xs_win = sb("xs_win", [P, TABLE], U8)
        gn_raw = sb("gn_raw", [P, PACK], F32)
        ws_raw = sb("ws_raw", [P, S], U8)
        w_raw = sb("w_raw", [P, 2 * S], U8)

        nc.gpsimd.memset(ds_win[:].bitcast(I32), 0)
        nc.vector.memset(xs_win[:].bitcast(I32), 0)
        nc.gpsimd.memset(ws_raw[:].bitcast(I32), 0)

        kidx_t = load_list("kidx_t", kidx)
        nc.sync.dma_start(ds_win[0:P:8, :].bitcast(I32), d_scales[0].bitcast(I32))
        nc.sync.dma_start(xs_win[0:P:8, :].bitcast(I32), x_scales[0].bitcast(I32))
        offs_t = load_list("offs_t", offs)
        n1_t = load_list("n1_t", n1)
        n2_t = load_list("n2_t", n2)
        nc.sync.dma_start(gn_raw[:], gn.rearrange("(p t) o -> p (t o)", t=PACK))
        nc.sync.dma_start(d_win[:].bitcast(I32), d_words[0].rearrange("p n t -> p (n t)").bitcast(I32))
        nc.sync.dma_start(x_win[:].bitcast(I32), x_words[0].rearrange("p n t -> p (n t)").bitcast(I32))
        nc.sync.dma_start(w_raw[:].bitcast(I32), w1_words[0].bitcast(I32))
        for q in range(4):
            nc.sync.dma_start(ws_raw[32 * q : 32 * q + 4, :].bitcast(I32), w1_scales[0, 4 * q : 4 * q + 4, :].bitcast(I32))
        n3_t = load_list("n3_t", n3)
        n5_t = load_list("n5_t", n5)
        n4_t = load_list("n4_t", n4)

        staged = sb("staged", [P, 2 * S], U8)
        planes = sb("planes", [P, 2 * S], U8)
        nc.vector.memset(planes[:].bitcast(I32), 0)
        d_plane = planes[:, 0:S]
        x_plane = planes[:, S : 2 * S]
        ds_got = sb("ds_got", [P, S], U8)
        nc.vector.tensor_copy(ds_got[:], ds_win[:].indirect(kidx_t[:]))
        xs_got = sb("xs_got", [P, S], U8)
        nc.vector.tensor_copy(xs_got[:], xs_win[:].indirect(offs_t[:]))
        nc.vector.tensor_copy(
            staged[:, 0:S].rearrange("p (t q) -> p q t", t=PACK), ds_got[:].rearrange("p (q t) -> p q t", t=PACK)
        )
        nc.vector.tensor_copy(staged[:, S : 2 * S].bitcast(I32), xs_got[:].bitcast(I32))
        for q in range(4):
            nc.scalar.dma_start(planes[32 * q : 32 * q + 4, :].bitcast(I32), staged[32 * q : 32 * (q + 1) : 8, :].bitcast(I32))

        d_got = sb("d_got", [P, S], U32)
        d_codes = sb("d_codes", [P, S], U32)
        nc.vector.tensor_copy(d_got[:], d_win[:].indirect(kidx_t[:]))
        dealt = d_codes[:].rearrange("p (t q) -> p q t", t=PACK)
        picked = d_got[:].rearrange("p (q t) -> p q t", t=PACK)

        gain = sb("gain", [P, PACK], F32)
        nc.scalar.activation(gain[:], gn_raw[:], COPY, scale=0.0625)

        x_codes = sb("x_codes", [P, S], U32)
        scores = [sb("score%d" % t, [P, S], F32) for t in range(PACK)]

        def score_matmul(bank, t, cols):
            keys = slice(t * P, (t + 1) * P)
            nc.tensor.matmul_mx(
                out=bank, lhsT=d_codes[:, keys].bitcast(FP8X4), lhsT_scale=d_plane[:, keys],
                rhs=x_codes[:, cols].bitcast(FP8X4), rhs_scale=x_plane[:, cols], start=True, stop=True,
            )

        chunks = (slice(0, 2 * CH), slice(2 * CH, 3 * CH), slice(3 * CH, S))
        for c, cols in enumerate(chunks):
            nc.vector.tensor_copy(x_codes[:, cols], x_win[:].indirect(offs_t[:, cols.start // 16 : cols.stop // 16]))
            if c == 0:
                nc.vector.tensor_copy(dealt[:, :, 0], picked[:, :, 0])
            bank = banks[c][:, 0 : cols.stop - cols.start]
            score_matmul(bank, 0, cols)
            nc.scalar.copy(scores[0][:, cols], bank)
        nc.vector.tensor_copy(dealt[:, :, 1:PACK], picked[:, :, 1:PACK])
        w_plane = sb("w_plane", [P, S], U8, tag="x_win")
        nc.vector.tensor_copy(
            w_plane[:].rearrange("p (t q) -> p q t", t=PACK), ws_raw[:].rearrange("p (q t) -> p q t", t=PACK)
        )

        for t in range(PACK):
            if t > 0:
                score_matmul(banks[2][:], t, slice(0, S))
                nc.scalar.copy(scores[t][:], banks[2][:])
            pa = sb("pa%d" % t, [P, W], F32)
            pb = sb("pb%d" % t, [P, W], F32)
            ra = sb("ra%d" % t, [P, W], F32)
            nc.scalar.activation(pa[:], scores[t][:].indirect(n1_t[:]), COPY)
            if t == 0:
                nc.vector.tensor_copy(pb[:], scores[t][:].indirect(n2_t[:]))
            else:
                nc.scalar.activation(pb[:], scores[t][:].indirect(n2_t[:]), COPY)
            nc.vector.tensor_tensor(ra[:], pa[:], pb[:], ALU.max)
            nc.vector.tensor_copy(scores[t][:].indirect(n1_t[:]), ra[:])

        pages = []
        for t in range(PACK):
            pages.append(sb("page%d" % t, [P, U], F32))

        w_codes = sb("w_codes", [P, 2 * S], U8)
        nc.scalar.copy(
            w_codes[:].bitcast(U16).rearrange("p (t q) -> p t q", t=PACK),
            w_raw[:].bitcast(U16).rearrange("p (q t) -> p t q", t=PACK),
        )

        chunks = (slice(0, CH), slice(CH, 2 * CH), slice(2 * CH, S))
        z_woven = [
            sb("z_woven%d" % c, [P, cols.stop - cols.start, PACK], BF16, tag="pb1" if c == 0 else "")
            for c, cols in enumerate(chunks)
        ]
        z_rest = sb("z_rest", [P, PACK, S - CH], BF16, tag="pa2")
        for t in range(PACK):
            g = gain[:, t : t + 1]
            nc.scalar.activation(z_woven[0][:, :, t], scores[t][:, 0:CH], COPY, scale=g)
            nc.scalar.activation(z_rest[:, t, :], scores[t][:, CH:S], COPY, scale=g)

        z_codes = sb("z_codes", [P, S], U32)
        z_plane = sb("z_plane", [P, S], U8)
        sums = [sb("sum%d" % t, [P, S], F32) for t in range(PACK)]

        def value_matmul(bank, t, cols):
            nc.tensor.matmul_mx(
                out=bank, lhsT=w_codes[:, 2 * t * P : 2 * (t + 1) * P].bitcast(FP4X4),
                lhsT_scale=w_plane[:, t * P : (t + 1) * P],
                rhs=z_codes[:, cols].bitcast(FP8X4), rhs_scale=z_plane[:, cols], start=True, stop=True,
            )

        for c, cols in enumerate(chunks):
            if c > 0:
                nc.scalar.copy(
                    z_woven[c][:].rearrange("p (j i) t -> p j t i", i=4),
                    z_rest[:, :, cols.start - CH : cols.stop - CH].rearrange("p t (j i) -> p j t i", i=4),
                )
            nc.vector.quantize_mx(
                out=z_codes[:, cols].bitcast(FP8X4), scales=z_plane[:, cols],
                in_=z_woven[c][:].rearrange("p j t -> p (j t)"),
            )
            for t in range(2):
                bank = banks[2 + 2 * c + t][:, 0 : cols.stop - cols.start]
                value_matmul(bank, t, cols)
                if c == 0 and t == 0:
                    nc.vector.tensor_copy(sums[t][:, cols], bank)
                else:
                    nc.scalar.copy(sums[t][:, cols], bank)
                nc.vector.tensor_copy(pages[t][:].indirect(n3_t[:, cols.start // 16 : cols.stop // 16]), sums[t][:, cols])

        out_rows = out.rearrange("(p t) w -> t p w", t=PACK)

        def second_fill(t):
            minus = sb("minus%d" % t, [P, S], F32)
            for half in range(2):
                nc.scalar.activation(
                    minus[:, half * W : (half + 1) * W],
                    sums[t][:].indirect(n5_t[:, half * 16 : (half + 1) * 16]), COPY, scale=-1.0,
                )
            nc.vector.tensor_tensor(pages[t][:].indirect(n4_t[:]), sums[t][:], minus[:], ALU.add)
            nc.sync.dma_start(out_rows[t], pages[t][:])

        for t in range(2, PACK):
            second_fill(t - 2)
            value_matmul(banks[t - 2][:], t, slice(0, S))
            nc.scalar.copy(sums[t][:], banks[t - 2][:])
            nc.vector.tensor_copy(pages[t][:].indirect(n3_t[:]), sums[t][:])
        second_fill(2)
        second_fill(3)
